import numpy as np
import ml_dtypes

BF16 = ml_dtypes.bfloat16


def bf(x):
    return np.asarray(x, np.float32).astype(BF16)


def f32(x):
    return np.asarray(x, np.float32)


def f64(x):
    return np.asarray(x).astype(np.float64)


def striped(idx):
    return np.tile(idx.reshape(-1, 16).T, (8, 1))


S, K, M, N = 512, 128, 256, 128


def gelu_tanh(v):
    return 0.5 * v * (1.0 + np.tanh(np.sqrt(2.0 / np.pi) * (v + 0.044715 * v**3)))


def setup_inputs():
    return {"base": bf(np.random.standard_normal((M, S))), "x": bf(np.random.standard_normal((K, N))), "w": bf(np.random.standard_normal((K, M)) / np.sqrt(K)), "b": f32(0.5 * np.random.standard_normal((M, 1))), "offs": striped(np.random.permutation(S)[:N])}


def reference(base, x, w, b, offs):
    idx = offs[:16].T.reshape(-1)
    z = f64(base).copy()
    z[:, idx] = f64(w).T @ f64(x)
    return gelu_tanh(z + f64(b))

@@ -1,0 +1,55 @@
+import concourse.mybir as mybir
+from concourse.masks import make_identity
+
+P = 128
+TOKENS = 512
+PICKED = 128
+FEATURES = 256
+BLOCKS = FEATURES // P
+
+FLOPS = 2 * P * FEATURES * PICKED
+
+BF16, F32, U16 = mybir.dt.bfloat16, mybir.dt.float32, mybir.dt.uint16
+GELU = mybir.ActivationFunctionType.Gelu_apprx_tanh
+
+
+def tile_scatter_matmul_kernel(tc, base, x, w, b, offs, out):
+    nc = tc.nc
+    with (
+        tc.tile_pool(name="held", bufs=1) as held,
+        tc.psum_pool(name="banks", bufs=1) as banks,
+    ):
+        base_tiles = [held.tile([P, TOKENS], BF16, name="base%d" % a) for a in range(BLOCKS)]
+        for a in range(BLOCKS):
+            nc.sync.dma_start(base_tiles[a][:], base[a * P : (a + 1) * P, :])
+        offsets = held.tile([P, PICKED // 16], U16, name="offsets")
+        nc.sync.dma_start(offsets[:], offs)
+
+        weights = held.tile([P, FEATURES], BF16, name="weights")
+        nc.scalar.dma_start(weights[:], w)
+        moving = held.tile([P, PICKED], BF16, name="moving")
+        nc.scalar.dma_start(moving[:], x)
+        bias = held.tile([P, BLOCKS], F32, name="bias")
+        with nc.allow_non_contiguous_dma(reason="one float32 to a partition for each block"):
+            nc.scalar.dma_start(bias[:], b.rearrange("(a p) o -> p (a o)", p=P))
+
+        identity = held.tile([P, P], BF16, name="identity")
+        make_identity(nc, identity[:])
+
+        windows = [banks.tile([P, TOKENS], F32, name="window%d" % a) for a in range(BLOCKS)]
+        for a in range(BLOCKS):
+            nc.tensor.matmul(windows[a][:], identity[:], base_tiles[a][:], start=True, stop=True)
+
+        for a in range(BLOCKS):
+            nc.tensor.matmul(
+                windows[a][:].indirect(offsets[:]),
+                weights[:, a * P : (a + 1) * P],
+                moving[:],
+                start=True,
+                stop=True,
+            )
+
+        for a in range(BLOCKS):
+            result = held.tile([P, TOKENS], F32, name="result%d" % a)
+            nc.scalar.activation(result[:], windows[a][:], GELU, bias=bias[:, a : a + 1])
+            nc.sync.dma_start(out[a * P : (a + 1) * P, :], result[:])

@@ -6,6 +6,7 @@ TOKENS = 512
 PICKED = 128
 FEATURES = 256
 BLOCKS = FEATURES // P
+PIECES = 2
 
 FLOPS = 2 * P * FEATURES * PICKED
 
@@ -22,16 +23,19 @@ def tile_scatter_matmul_kernel(tc, base, x, w, b, offs, out):
         base_tiles = [held.tile([P, TOKENS], BF16, name="base%d" % a) for a in range(BLOCKS)]
         for a in range(BLOCKS):
             nc.sync.dma_start(base_tiles[a][:], base[a * P : (a + 1) * P, :])
+        weights = held.tile([P, FEATURES], BF16, name="weights")
+        nc.sync.dma_start(weights[:], w)
+        moving = held.tile([P, PICKED], BF16, name="moving")
+        nc.sync.dma_start(moving[:], x)
         offsets = held.tile([P, PICKED // 16], U16, name="offsets")
         nc.sync.dma_start(offsets[:], offs)
-
-        weights = held.tile([P, FEATURES], BF16, name="weights")
-        nc.scalar.dma_start(weights[:], w)
-        moving = held.tile([P, PICKED], BF16, name="moving")
-        nc.scalar.dma_start(moving[:], x)
         bias = held.tile([P, BLOCKS], F32, name="bias")
         with nc.allow_non_contiguous_dma(reason="one float32 to a partition for each block"):
-            nc.scalar.dma_start(bias[:], b.rearrange("(a p) o -> p (a o)", p=P))
+            nc.sync.dma_start(bias[:], b.rearrange("(a p) o -> p (a o)", p=P))
+
+        warm = held.tile([P, 1], F32, name="warm")
+        nc.vector.memset(warm[:], 0.0)
+        nc.scalar.activation(warm[:], warm[:], GELU)
 
         identity = held.tile([P, P], BF16, name="identity")
         make_identity(nc, identity[:])
@@ -50,6 +54,8 @@ def tile_scatter_matmul_kernel(tc, base, x, w, b, offs, out):
             )
 
         for a in range(BLOCKS):
-            result = held.tile([P, TOKENS], F32, name="result%d" % a)
-            nc.scalar.activation(result[:], windows[a][:], GELU, bias=bias[:, a : a + 1])
-            nc.sync.dma_start(out[a * P : (a + 1) * P, :], result[:])
+            for c in range(0, TOKENS, TOKENS // PIECES):
+                columns = slice(c, c + TOKENS // PIECES)
+                result = held.tile([P, TOKENS // PIECES], F32, name="result%d_%d" % (a, c))
+                nc.scalar.activation(result[:], windows[a][:, columns], GELU, bias=bias[:, a : a + 1])
+                nc.sync.dma_start(out[a * P : (a + 1) * P, columns], result[:])

@@ -7,6 +7,8 @@ PICKED = 128
 FEATURES = 256
 BLOCKS = FEATURES // P
 PIECES = 2
+WARM_COLUMNS = 256
+WARM_MATMULS = 5
 
 FLOPS = 2 * P * FEATURES * PICKED
 
@@ -32,6 +34,12 @@ def tile_scatter_matmul_kernel(tc, base, x, w, b, offs, out):
         bias = held.tile([P, BLOCKS], F32, name="bias")
         with nc.allow_non_contiguous_dma(reason="one float32 to a partition for each block"):
             nc.sync.dma_start(bias[:], b.rearrange("(a p) o -> p (a o)", p=P))
+
+        zeros = held.tile([P, WARM_COLUMNS], BF16, name="zeros")
+        nc.vector.memset(zeros[:], 0.0)
+        spare = banks.tile([P, WARM_COLUMNS], F32, name="spare")
+        for i in range(WARM_MATMULS):
+            nc.tensor.matmul(spare[:], zeros[:, 0:P], zeros[:], start=True, stop=True)
 
         warm = held.tile([P, 1], F32, name="warm")
         nc.vector.memset(warm[:], 0.0)

@@ -7,8 +7,6 @@ PICKED = 128
 FEATURES = 256
 BLOCKS = FEATURES // P
 PIECES = 2
-WARM_COLUMNS = 256
-WARM_MATMULS = 5
 
 FLOPS = 2 * P * FEATURES * PICKED
 
@@ -22,6 +20,10 @@ def tile_scatter_matmul_kernel(tc, base, x, w, b, offs, out):
         tc.tile_pool(name="held", bufs=1) as held,
         tc.psum_pool(name="banks", bufs=1) as banks,
     ):
+        bias = held.tile([P, BLOCKS], F32, name="bias")
+        with nc.allow_non_contiguous_dma(reason="one float32 to a partition for each block"):
+            nc.scalar.dma_start(bias[:], b.rearrange("(a p) o -> p (a o)", p=P))
+
         base_tiles = [held.tile([P, TOKENS], BF16, name="base%d" % a) for a in range(BLOCKS)]
         for a in range(BLOCKS):
             nc.sync.dma_start(base_tiles[a][:], base[a * P : (a + 1) * P, :])
@@ -31,15 +33,6 @@ def tile_scatter_matmul_kernel(tc, base, x, w, b, offs, out):
         nc.sync.dma_start(moving[:], x)
         offsets = held.tile([P, PICKED // 16], U16, name="offsets")
         nc.sync.dma_start(offsets[:], offs)
-        bias = held.tile([P, BLOCKS], F32, name="bias")
-        with nc.allow_non_contiguous_dma(reason="one float32 to a partition for each block"):
-            nc.sync.dma_start(bias[:], b.rearrange("(a p) o -> p (a o)", p=P))
-
-        zeros = held.tile([P, WARM_COLUMNS], BF16, name="zeros")
-        nc.vector.memset(zeros[:], 0.0)
-        spare = banks.tile([P, WARM_COLUMNS], F32, name="spare")
-        for i in range(WARM_MATMULS):
-            nc.tensor.matmul(spare[:], zeros[:, 0:P], zeros[:], start=True, stop=True)
 
         warm = held.tile([P, 1], F32, name="warm")
         nc.vector.memset(warm[:], 0.0)

@@ -20,19 +20,20 @@ def tile_scatter_matmul_kernel(tc, base, x, w, b, offs, out):
         tc.tile_pool(name="held", bufs=1) as held,
         tc.psum_pool(name="banks", bufs=1) as banks,
     ):
-        bias = held.tile([P, BLOCKS], F32, name="bias")
-        with nc.allow_non_contiguous_dma(reason="one float32 to a partition for each block"):
-            nc.scalar.dma_start(bias[:], b.rearrange("(a p) o -> p (a o)", p=P))
-
-        base_tiles = [held.tile([P, TOKENS], BF16, name="base%d" % a) for a in range(BLOCKS)]
+        base_tiles = {}
         for a in range(BLOCKS):
-            nc.sync.dma_start(base_tiles[a][:], base[a * P : (a + 1) * P, :])
+            for c in range(0, TOKENS, TOKENS // PIECES):
+                base_tiles[a, c] = held.tile([P, TOKENS // PIECES], BF16, name="base%d_%d" % (a, c))
+                nc.sync.dma_start(base_tiles[a, c][:], base[a * P : (a + 1) * P, c : c + TOKENS // PIECES])
         weights = held.tile([P, FEATURES], BF16, name="weights")
         nc.sync.dma_start(weights[:], w)
         moving = held.tile([P, PICKED], BF16, name="moving")
         nc.sync.dma_start(moving[:], x)
         offsets = held.tile([P, PICKED // 16], U16, name="offsets")
         nc.sync.dma_start(offsets[:], offs)
+        bias = held.tile([P, BLOCKS], F32, name="bias")
+        with nc.allow_non_contiguous_dma(reason="one float32 to a partition for each block"):
+            nc.sync.dma_start(bias[:], b.rearrange("(a p) o -> p (a o)", p=P))
 
         warm = held.tile([P, 1], F32, name="warm")
         nc.vector.memset(warm[:], 0.0)
@@ -43,7 +44,10 @@ def tile_scatter_matmul_kernel(tc, base, x, w, b, offs, out):
 
         windows = [banks.tile([P, TOKENS], F32, name="window%d" % a) for a in range(BLOCKS)]
         for a in range(BLOCKS):
-            nc.tensor.matmul(windows[a][:], identity[:], base_tiles[a][:], start=True, stop=True)
+            for c in range(0, TOKENS, TOKENS // PIECES):
+                nc.tensor.matmul(
+                    windows[a][:, c : c + TOKENS // PIECES], identity[:], base_tiles[a, c][:], start=True, stop=True
+                )
 
         for a in range(BLOCKS):
             nc.tensor.matmul(

@@ -7,6 +7,7 @@ PICKED = 128
 FEATURES = 256
 BLOCKS = FEATURES // P
 PIECES = 2
+IDLE_MATMULS = 8
 
 FLOPS = 2 * P * FEATURES * PICKED
 
@@ -35,9 +36,15 @@ def tile_scatter_matmul_kernel(tc, base, x, w, b, offs, out):
         with nc.allow_non_contiguous_dma(reason="one float32 to a partition for each block"):
             nc.sync.dma_start(bias[:], b.rearrange("(a p) o -> p (a o)", p=P))
 
+        zeros = held.tile([P, P], BF16, name="zeros")
+        nc.vector.memset(zeros[:], 0.0)
+
         warm = held.tile([P, 1], F32, name="warm")
-        nc.vector.memset(warm[:], 0.0)
-        nc.scalar.activation(warm[:], warm[:], GELU)
+        nc.scalar.activation(warm[:], zeros[:, 0:1], GELU)
+
+        spare = banks.tile([P, P], F32, name="spare")
+        for i in range(IDLE_MATMULS):
+            nc.tensor.matmul(spare[:], zeros[:], zeros[:], start=True, stop=True)
 
         identity = held.tile([P, P], BF16, name="identity")
         make_identity(nc, identity[:])

@@ -7,6 +7,7 @@ PICKED = 128
 FEATURES = 256
 BLOCKS = FEATURES // P
 PIECES = 2
+TURN = 32
 IDLE_MATMULS = 8
 
 FLOPS = 2 * P * FEATURES * PICKED
@@ -21,6 +22,11 @@ def tile_scatter_matmul_kernel(tc, base, x, w, b, offs, out):
         tc.tile_pool(name="held", bufs=1) as held,
         tc.psum_pool(name="banks", bufs=1) as banks,
     ):
+        zeros = held.tile([P, P], BF16, name="zeros")
+        nc.vector.memset(zeros[:], 0.0)
+        bias_runs = held.tile([P, BLOCKS * TURN], F32, name="bias_runs", align_bytes=64)
+        nc.vector.memset(bias_runs[:], 0.0)
+
         base_tiles = {}
         for a in range(BLOCKS):
             for c in range(0, TOKENS, TOKENS // PIECES):
@@ -32,12 +38,13 @@ def tile_scatter_matmul_kernel(tc, base, x, w, b, offs, out):
         nc.sync.dma_start(moving[:], x)
         offsets = held.tile([P, PICKED // 16], U16, name="offsets")
         nc.sync.dma_start(offsets[:], offs)
-        bias = held.tile([P, BLOCKS], F32, name="bias")
-        with nc.allow_non_contiguous_dma(reason="one float32 to a partition for each block"):
-            nc.sync.dma_start(bias[:], b.rearrange("(a p) o -> p (a o)", p=P))
-
-        zeros = held.tile([P, P], BF16, name="zeros")
-        nc.vector.memset(zeros[:], 0.0)
+        nc.sync.dma_start(
+            bias_runs[0:P:TURN, :].rearrange("q (a i) -> q a i", a=BLOCKS),
+            b.rearrange("(a q i) o -> q a (i o)", a=BLOCKS, i=TURN),
+        )
+        bias = held.tile([P, BLOCKS * TURN], F32, name="bias", align_bytes=64)
+        for a in range(BLOCKS):
+            nc.vector.transpose(bias[:, a * TURN : (a + 1) * TURN], bias_runs[:, a * TURN : (a + 1) * TURN])
 
         warm = held.tile([P, 1], F32, name="warm")
         nc.scalar.activation(warm[:], zeros[:, 0:1], GELU)
@@ -69,5 +76,5 @@ def tile_scatter_matmul_kernel(tc, base, x, w, b, offs, out):
             for c in range(0, TOKENS, TOKENS // PIECES):
                 columns = slice(c, c + TOKENS // PIECES)
                 result = held.tile([P, TOKENS // PIECES], F32, name="result%d_%d" % (a, c))
-                nc.scalar.activation(result[:], windows[a][:, columns], GELU, bias=bias[:, a : a + 1])
+                nc.scalar.activation(result[:], windows[a][:, columns], GELU, bias=bias[:, a * TURN : a * TURN + 1])
                 nc.sync.dma_start(out[a * P : (a + 1) * P, columns], result[:])

@@ -29,9 +29,10 @@ def tile_scatter_matmul_kernel(tc, base, x, w, b, offs, out):
 
         base_tiles = {}
         for a in range(BLOCKS):
-            for c in range(0, TOKENS, TOKENS // PIECES):
-                base_tiles[a, c] = held.tile([P, TOKENS // PIECES], BF16, name="base%d_%d" % (a, c))
-                nc.sync.dma_start(base_tiles[a, c][:], base[a * P : (a + 1) * P, c : c + TOKENS // PIECES])
+            width = TOKENS // PIECES if a == 0 else TOKENS
+            for c in range(0, TOKENS, width):
+                base_tiles[a, c] = held.tile([P, width], BF16, name="base%d_%d" % (a, c))
+                nc.sync.dma_start(base_tiles[a, c][:], base[a * P : (a + 1) * P, c : c + width])
         weights = held.tile([P, FEATURES], BF16, name="weights")
         nc.sync.dma_start(weights[:], w)
         moving = held.tile([P, PICKED], BF16, name="moving")
@@ -57,11 +58,8 @@ def tile_scatter_matmul_kernel(tc, base, x, w, b, offs, out):
         make_identity(nc, identity[:])
 
         windows = [banks.tile([P, TOKENS], F32, name="window%d" % a) for a in range(BLOCKS)]
-        for a in range(BLOCKS):
-            for c in range(0, TOKENS, TOKENS // PIECES):
-                nc.tensor.matmul(
-                    windows[a][:, c : c + TOKENS // PIECES], identity[:], base_tiles[a, c][:], start=True, stop=True
-                )
+        for (a, c), piece in base_tiles.items():
+            nc.tensor.matmul(windows[a][:, c : c + piece.shape[1]], identity[:], piece[:], start=True, stop=True)
 
         for a in range(BLOCKS):
             nc.tensor.matmul(

@@ -8,6 +8,7 @@ FEATURES = 256
 BLOCKS = FEATURES // P
 PIECES = 2
 TURN = 32
+LINE = 256
 IDLE_MATMULS = 8
 
 FLOPS = 2 * P * FEATURES * PICKED
@@ -24,20 +25,20 @@ def tile_scatter_matmul_kernel(tc, base, x, w, b, offs, out):
     ):
         zeros = held.tile([P, P], BF16, name="zeros")
         nc.vector.memset(zeros[:], 0.0)
-        bias_runs = held.tile([P, BLOCKS * TURN], F32, name="bias_runs", align_bytes=64)
+        bias_runs = held.tile([P, BLOCKS * TURN], F32, name="bias_runs", align_bytes=LINE)
         nc.vector.memset(bias_runs[:], 0.0)
 
         base_tiles = {}
         for a in range(BLOCKS):
             width = TOKENS // PIECES if a == 0 else TOKENS
             for c in range(0, TOKENS, width):
-                base_tiles[a, c] = held.tile([P, width], BF16, name="base%d_%d" % (a, c))
+                base_tiles[a, c] = held.tile([P, width], BF16, name="base%d_%d" % (a, c), align_bytes=LINE)
                 nc.sync.dma_start(base_tiles[a, c][:], base[a * P : (a + 1) * P, c : c + width])
-        weights = held.tile([P, FEATURES], BF16, name="weights")
+        weights = held.tile([P, FEATURES], BF16, name="weights", align_bytes=LINE)
         nc.sync.dma_start(weights[:], w)
-        moving = held.tile([P, PICKED], BF16, name="moving")
+        moving = held.tile([P, PICKED], BF16, name="moving", align_bytes=LINE)
         nc.sync.dma_start(moving[:], x)
-        offsets = held.tile([P, PICKED // 16], U16, name="offsets")
+        offsets = held.tile([P, PICKED // 16], U16, name="offsets", align_bytes=LINE)
         nc.sync.dma_start(offsets[:], offs)
         nc.sync.dma_start(
             bias_runs[0:P:TURN, :].rearrange("q (a i) -> q a i", a=BLOCKS),
@@ -73,6 +74,6 @@ def tile_scatter_matmul_kernel(tc, base, x, w, b, offs, out):
         for a in range(BLOCKS):
             for c in range(0, TOKENS, TOKENS // PIECES):
                 columns = slice(c, c + TOKENS // PIECES)
-                result = held.tile([P, TOKENS // PIECES], F32, name="result%d_%d" % (a, c))
+                result = held.tile([P, TOKENS // PIECES], F32, name="result%d_%d" % (a, c), align_bytes=LINE)
                 nc.scalar.activation(result[:], windows[a][:, columns], GELU, bias=bias[:, a * TURN : a * TURN + 1])
                 nc.sync.dma_start(out[a * P : (a + 1) * P, columns], result[:])

@@ -10,6 +10,8 @@ PIECES = 2
 TURN = 32
 LINE = 256
 IDLE_MATMULS = 8
+BETWEEN_RUNS = 24
+UNIT = 16
 
 FLOPS = 2 * P * FEATURES * PICKED
 
@@ -28,12 +30,10 @@ def tile_scatter_matmul_kernel(tc, base, x, w, b, offs, out):
         bias_runs = held.tile([P, BLOCKS * TURN], F32, name="bias_runs", align_bytes=LINE)
         nc.vector.memset(bias_runs[:], 0.0)
 
-        base_tiles = {}
-        for a in range(BLOCKS):
-            width = TOKENS // PIECES if a == 0 else TOKENS
-            for c in range(0, TOKENS, width):
-                base_tiles[a, c] = held.tile([P, width], BF16, name="base%d_%d" % (a, c), align_bytes=LINE)
-                nc.sync.dma_start(base_tiles[a, c][:], base[a * P : (a + 1) * P, c : c + width])
+        first_pieces = {}
+        for c in range(0, TOKENS, TOKENS // PIECES):
+            first_pieces[c] = held.tile([P, TOKENS // PIECES], BF16, name="base0_%d" % c, align_bytes=LINE)
+            nc.sync.dma_start(first_pieces[c][:], base[0:P, c : c + TOKENS // PIECES])
         weights = held.tile([P, FEATURES], BF16, name="weights", align_bytes=LINE)
         nc.sync.dma_start(weights[:], w)
         moving = held.tile([P, PICKED], BF16, name="moving", align_bytes=LINE)
@@ -44,6 +44,11 @@ def tile_scatter_matmul_kernel(tc, base, x, w, b, offs, out):
             bias_runs[0:P:TURN, :].rearrange("q (a i) -> q a i", a=BLOCKS),
             b.rearrange("(a q i) o -> q a (i o)", a=BLOCKS, i=TURN),
         )
+        later_rows = {}
+        for a in range(1, BLOCKS):
+            later_rows[a] = held.tile([P, TOKENS], BF16, name="base%d" % a, align_bytes=LINE)
+            nc.sync.dma_start(later_rows[a][:], base[a * P : (a + 1) * P, :])
+
         bias = held.tile([P, BLOCKS * TURN], F32, name="bias", align_bytes=64)
         for a in range(BLOCKS):
             nc.vector.transpose(bias[:, a * TURN : (a + 1) * TURN], bias_runs[:, a * TURN : (a + 1) * TURN])
@@ -59,10 +64,14 @@ def tile_scatter_matmul_kernel(tc, base, x, w, b, offs, out):
         make_identity(nc, identity[:])
 
         windows = [banks.tile([P, TOKENS], F32, name="window%d" % a) for a in range(BLOCKS)]
-        for (a, c), piece in base_tiles.items():
-            nc.tensor.matmul(windows[a][:, c : c + piece.shape[1]], identity[:], piece[:], start=True, stop=True)
-
         for a in range(BLOCKS):
+            if a == 0:
+                for c, piece in first_pieces.items():
+                    nc.tensor.matmul(windows[a][:, c : c + TOKENS // PIECES], identity[:], piece[:], start=True, stop=True)
+            else:
+                edges = [UNIT * (TOKENS // UNIT * i // BETWEEN_RUNS) for i in range(BETWEEN_RUNS + 1)]
+                for lo, hi in zip(edges[:-1], edges[1:]):
+                    nc.tensor.matmul(windows[a][:, lo:hi], identity[:], later_rows[a][:, lo:hi], start=True, stop=True)
             nc.tensor.matmul(
                 windows[a][:].indirect(offsets[:]),
                 weights[:, a * P : (a + 1) * P],
@@ -70,8 +79,6 @@ def tile_scatter_matmul_kernel(tc, base, x, w, b, offs, out):
                 start=True,
                 stop=True,
             )
-
-        for a in range(BLOCKS):
             for c in range(0, TOKENS, TOKENS // PIECES):
                 columns = slice(c, c + TOKENS // PIECES)
                 result = held.tile([P, TOKENS // PIECES], F32, name="result%d_%d" % (a, c), align_bytes=LINE)

@@ -30,24 +30,26 @@ def tile_scatter_matmul_kernel(tc, base, x, w, b, offs, out):
         bias_runs = held.tile([P, BLOCKS * TURN], F32, name="bias_runs", align_bytes=LINE)
         nc.vector.memset(bias_runs[:], 0.0)
 
-        first_pieces = {}
-        for c in range(0, TOKENS, TOKENS // PIECES):
-            first_pieces[c] = held.tile([P, TOKENS // PIECES], BF16, name="base0_%d" % c, align_bytes=LINE)
-            nc.sync.dma_start(first_pieces[c][:], base[0:P, c : c + TOKENS // PIECES])
+        def load_rows(a, pieces):
+            tiles = {}
+            for c in range(0, TOKENS, TOKENS // pieces):
+                tiles[c] = held.tile([P, TOKENS // pieces], BF16, name="base%d_%d" % (a, c), align_bytes=LINE)
+                nc.sync.dma_start(tiles[c][:], base[a * P : (a + 1) * P, c : c + TOKENS // pieces])
+            return tiles
+
+        rows = {0: load_rows(0, 1)}
         weights = held.tile([P, FEATURES], BF16, name="weights", align_bytes=LINE)
         nc.sync.dma_start(weights[:], w)
         moving = held.tile([P, PICKED], BF16, name="moving", align_bytes=LINE)
         nc.sync.dma_start(moving[:], x)
-        offsets = held.tile([P, PICKED // 16], U16, name="offsets", align_bytes=LINE)
-        nc.sync.dma_start(offsets[:], offs)
         nc.sync.dma_start(
             bias_runs[0:P:TURN, :].rearrange("q (a i) -> q a i", a=BLOCKS),
             b.rearrange("(a q i) o -> q a (i o)", a=BLOCKS, i=TURN),
         )
-        later_rows = {}
+        offsets = held.tile([P, PICKED // 16], U16, name="offsets", align_bytes=LINE)
+        nc.sync.dma_start(offsets[:], offs)
         for a in range(1, BLOCKS):
-            later_rows[a] = held.tile([P, TOKENS], BF16, name="base%d" % a, align_bytes=LINE)
-            nc.sync.dma_start(later_rows[a][:], base[a * P : (a + 1) * P, :])
+            rows[a] = load_rows(a, PIECES)
 
         bias = held.tile([P, BLOCKS * TURN], F32, name="bias", align_bytes=64)
         for a in range(BLOCKS):
@@ -65,13 +67,12 @@ def tile_scatter_matmul_kernel(tc, base, x, w, b, offs, out):
 
         windows = [banks.tile([P, TOKENS], F32, name="window%d" % a) for a in range(BLOCKS)]
         for a in range(BLOCKS):
-            if a == 0:
-                for c, piece in first_pieces.items():
-                    nc.tensor.matmul(windows[a][:, c : c + TOKENS // PIECES], identity[:], piece[:], start=True, stop=True)
-            else:
-                edges = [UNIT * (TOKENS // UNIT * i // BETWEEN_RUNS) for i in range(BETWEEN_RUNS + 1)]
+            cuts = 1 if a == 0 else BETWEEN_RUNS // PIECES
+            for c, piece in rows[a].items():
+                units = piece.shape[1] // UNIT
+                edges = [UNIT * (units * i // cuts) for i in range(cuts + 1)]
                 for lo, hi in zip(edges[:-1], edges[1:]):
-                    nc.tensor.matmul(windows[a][:, lo:hi], identity[:], later_rows[a][:, lo:hi], start=True, stop=True)
+                    nc.tensor.matmul(windows[a][:, c + lo : c + hi], identity[:], piece[:, lo:hi], start=True, stop=True)
             nc.tensor.matmul(
                 windows[a][:].indirect(offsets[:]),
                 weights[:, a * P : (a + 1) * P],

@@ -9,7 +9,7 @@ BLOCKS = FEATURES // P
 PIECES = 2
 TURN = 32
 LINE = 256
-IDLE_MATMULS = 8
+IDLE_MATMULS = 2
 BETWEEN_RUNS = 24
 UNIT = 16
 
@@ -25,10 +25,13 @@ def tile_scatter_matmul_kernel(tc, base, x, w, b, offs, out):
         tc.tile_pool(name="held", bufs=1) as held,
         tc.psum_pool(name="banks", bufs=1) as banks,
     ):
-        zeros = held.tile([P, P], BF16, name="zeros")
+        zeros = held.tile([P, TURN], BF16, name="zeros")
         nc.vector.memset(zeros[:], 0.0)
         bias_runs = held.tile([P, BLOCKS * TURN], F32, name="bias_runs", align_bytes=LINE)
         nc.vector.memset(bias_runs[:], 0.0)
+        identity = held.tile([P, P], BF16, name="identity")
+        nc.vector.memset(identity[:], 0.0)
+        make_identity(nc, identity[:], nomemset=True)
 
         def load_rows(a, pieces):
             tiles = {}
@@ -58,12 +61,9 @@ def tile_scatter_matmul_kernel(tc, base, x, w, b, offs, out):
         warm = held.tile([P, 1], F32, name="warm")
         nc.scalar.activation(warm[:], zeros[:, 0:1], GELU)
 
-        spare = banks.tile([P, P], F32, name="spare")
+        spare = banks.tile([TURN, TOKENS], F32, name="spare")
         for i in range(IDLE_MATMULS):
-            nc.tensor.matmul(spare[:], zeros[:], zeros[:], start=True, stop=True)
-
-        identity = held.tile([P, P], BF16, name="identity")
-        make_identity(nc, identity[:])
+            nc.tensor.matmul(spare[:], zeros[:], zeros[:, 0:1].to_broadcast([P, TOKENS]), start=True, stop=True)
 
         windows = [banks.tile([P, TOKENS], F32, name="window%d" % a) for a in range(BLOCKS)]
         for a in range(BLOCKS):

@@ -67,12 +67,23 @@ def tile_scatter_matmul_kernel(tc, base, x, w, b, offs, out):
 
         windows = [banks.tile([P, TOKENS], F32, name="window%d" % a) for a in range(BLOCKS)]
         for a in range(BLOCKS):
-            cuts = 1 if a == 0 else BETWEEN_RUNS // PIECES
-            for c, piece in rows[a].items():
-                units = piece.shape[1] // UNIT
-                edges = [UNIT * (units * i // cuts) for i in range(cuts + 1)]
-                for lo, hi in zip(edges[:-1], edges[1:]):
-                    nc.tensor.matmul(windows[a][:, c + lo : c + hi], identity[:], piece[:, lo:hi], start=True, stop=True)
+            if a == 0:
+                for c, piece in rows[a].items():
+                    nc.tensor.matmul(windows[a][:, c : c + piece.shape[1]], identity[:], piece[:], start=True, stop=True)
+            else:
+                cuts = BETWEEN_RUNS // (P // TURN) // PIECES
+                for c, piece in rows[a].items():
+                    units = piece.shape[1] // UNIT
+                    edges = [UNIT * (units * i // cuts) for i in range(cuts + 1)]
+                    for lo, hi in zip(edges[:-1], edges[1:]):
+                        for q in range(0, P, TURN):
+                            nc.tensor.matmul(
+                                windows[a][q : q + TURN, c + lo : c + hi],
+                                identity[:, q : q + TURN],
+                                piece[:, lo:hi],
+                                start=True,
+                                stop=True,
+                            )
             nc.tensor.matmul(
                 windows[a][:].indirect(offsets[:]),
                 weights[:, a * P : (a + 1) * P],

@@ -40,19 +40,23 @@ def tile_scatter_matmul_kernel(tc, base, x, w, b, offs, out):
                 nc.sync.dma_start(tiles[c][:], base[a * P : (a + 1) * P, c : c + TOKENS // pieces])
             return tiles
 
+        def load_bias(a):
+            nc.sync.dma_start(
+                bias_runs[0:P:TURN, a * TURN : (a + 1) * TURN],
+                b[a * P : (a + 1) * P, :].rearrange("(q i) o -> q (i o)", i=TURN),
+            )
+
         rows = {0: load_rows(0, 1)}
         weights = held.tile([P, FEATURES], BF16, name="weights", align_bytes=LINE)
         nc.sync.dma_start(weights[:], w)
         moving = held.tile([P, PICKED], BF16, name="moving", align_bytes=LINE)
         nc.sync.dma_start(moving[:], x)
-        nc.sync.dma_start(
-            bias_runs[0:P:TURN, :].rearrange("q (a i) -> q a i", a=BLOCKS),
-            b.rearrange("(a q i) o -> q a (i o)", a=BLOCKS, i=TURN),
-        )
+        load_bias(0)
         offsets = held.tile([P, PICKED // 16], U16, name="offsets", align_bytes=LINE)
         nc.sync.dma_start(offsets[:], offs)
         for a in range(1, BLOCKS):
             rows[a] = load_rows(a, PIECES)
+            load_bias(a)
 
         bias = held.tile([P, BLOCKS * TURN], F32, name="bias", align_bytes=64)
         for a in range(BLOCKS):

@@ -25,10 +25,10 @@ def tile_scatter_matmul_kernel(tc, base, x, w, b, offs, out):
         tc.tile_pool(name="held", bufs=1) as held,
         tc.psum_pool(name="banks", bufs=1) as banks,
     ):
-        zeros = held.tile([P, TURN], BF16, name="zeros")
-        nc.vector.memset(zeros[:], 0.0)
         bias_runs = held.tile([P, BLOCKS * TURN], F32, name="bias_runs", align_bytes=LINE)
         nc.vector.memset(bias_runs[:], 0.0)
+        zeros = held.tile([P, TURN], BF16, name="zeros")
+        nc.vector.memset(zeros[:], 0.0)
         identity = held.tile([P, P], BF16, name="identity")
         nc.vector.memset(identity[:], 0.0)
         make_identity(nc, identity[:], nomemset=True)
@@ -40,23 +40,23 @@ def tile_scatter_matmul_kernel(tc, base, x, w, b, offs, out):
                 nc.sync.dma_start(tiles[c][:], base[a * P : (a + 1) * P, c : c + TOKENS // pieces])
             return tiles
 
-        def load_bias(a):
-            nc.sync.dma_start(
+        def load_bias(a, queue):
+            queue.dma_start(
                 bias_runs[0:P:TURN, a * TURN : (a + 1) * TURN],
                 b[a * P : (a + 1) * P, :].rearrange("(q i) o -> q (i o)", i=TURN),
             )
 
+        load_bias(0, nc.scalar)
         rows = {0: load_rows(0, 1)}
         weights = held.tile([P, FEATURES], BF16, name="weights", align_bytes=LINE)
         nc.sync.dma_start(weights[:], w)
         moving = held.tile([P, PICKED], BF16, name="moving", align_bytes=LINE)
         nc.sync.dma_start(moving[:], x)
-        load_bias(0)
         offsets = held.tile([P, PICKED // 16], U16, name="offsets", align_bytes=LINE)
         nc.sync.dma_start(offsets[:], offs)
         for a in range(1, BLOCKS):
             rows[a] = load_rows(a, PIECES)
-            load_bias(a)
+            load_bias(a, nc.sync)
 
         bias = held.tile([P, BLOCKS * TURN], F32, name="bias", align_bytes=64)
         for a in range(BLOCKS):

@@ -33,12 +33,17 @@ def tile_scatter_matmul_kernel(tc, base, x, w, b, offs, out):
         nc.vector.memset(identity[:], 0.0)
         make_identity(nc, identity[:], nomemset=True)
 
-        def load_rows(a, pieces):
+        def load_rows(a):
             tiles = {}
-            for c in range(0, TOKENS, TOKENS // pieces):
-                tiles[c] = held.tile([P, TOKENS // pieces], BF16, name="base%d_%d" % (a, c), align_bytes=LINE)
-                nc.sync.dma_start(tiles[c][:], base[a * P : (a + 1) * P, c : c + TOKENS // pieces])
+            for c in range(0, TOKENS, TOKENS // PIECES):
+                tiles[c] = held.tile([P, TOKENS // PIECES], BF16, name="base%d_%d" % (a, c), align_bytes=LINE)
+                nc.sync.dma_start(tiles[c][:], base[a * P : (a + 1) * P, c : c + TOKENS // PIECES])
             return tiles
+
+        def load_weights(a):
+            block = held.tile([P, P], BF16, name="weights%d" % a, align_bytes=LINE)
+            nc.sync.dma_start(block[:], w[:, a * P : (a + 1) * P])
+            return block
 
         def load_bias(a, queue):
             queue.dma_start(
@@ -47,15 +52,15 @@ def tile_scatter_matmul_kernel(tc, base, x, w, b, offs, out):
             )
 
         load_bias(0, nc.scalar)
-        rows = {0: load_rows(0, 1)}
-        weights = held.tile([P, FEATURES], BF16, name="weights", align_bytes=LINE)
-        nc.sync.dma_start(weights[:], w)
+        rows = {0: load_rows(0)}
+        weights = {0: load_weights(0)}
         moving = held.tile([P, PICKED], BF16, name="moving", align_bytes=LINE)
         nc.sync.dma_start(moving[:], x)
         offsets = held.tile([P, PICKED // 16], U16, name="offsets", align_bytes=LINE)
         nc.sync.dma_start(offsets[:], offs)
         for a in range(1, BLOCKS):
-            rows[a] = load_rows(a, PIECES)
+            rows[a] = load_rows(a)
+            weights[a] = load_weights(a)
             load_bias(a, nc.sync)
 
         bias = held.tile([P, BLOCKS * TURN], F32, name="bias", align_bytes=64)
@@ -90,7 +95,7 @@ def tile_scatter_matmul_kernel(tc, base, x, w, b, offs, out):
                             )
             nc.tensor.matmul(
                 windows[a][:].indirect(offsets[:]),
-                weights[:, a * P : (a + 1) * P],
+                weights[a][:],
                 moving[:],
                 start=True,
                 stop=True,

import concourse.mybir as mybir
from concourse.masks import make_identity

P = 128
TOKENS = 512
PICKED = 128
FEATURES = 256
BLOCKS = FEATURES // P
PIECES = 2
TURN = 32
LINE = 256
IDLE_MATMULS = 2
BETWEEN_RUNS = 24
UNIT = 16

FLOPS = 2 * P * FEATURES * PICKED

BF16, F32, U16 = mybir.dt.bfloat16, mybir.dt.float32, mybir.dt.uint16
GELU = mybir.ActivationFunctionType.Gelu_apprx_tanh


def tile_scatter_matmul_kernel(tc, base, x, w, b, offs, out):
    nc = tc.nc
    with (
        tc.tile_pool(name="held", bufs=1) as held,
        tc.psum_pool(name="banks", bufs=1) as banks,
    ):
        bias_runs = held.tile([P, BLOCKS * TURN], F32, name="bias_runs", align_bytes=LINE)
        nc.vector.memset(bias_runs[:], 0.0)
        zeros = held.tile([P, TURN], BF16, name="zeros")
        nc.vector.memset(zeros[:], 0.0)
        identity = held.tile([P, P], BF16, name="identity")
        nc.vector.memset(identity[:], 0.0)
        make_identity(nc, identity[:], nomemset=True)

        def load_rows(a):
            tiles = {}
            for c in range(0, TOKENS, TOKENS // PIECES):
                tiles[c] = held.tile([P, TOKENS // PIECES], BF16, name="base%d_%d" % (a, c), align_bytes=LINE)
                nc.sync.dma_start(tiles[c][:], base[a * P : (a + 1) * P, c : c + TOKENS // PIECES])
            return tiles

        def load_weights(a):
            block = held.tile([P, P], BF16, name="weights%d" % a, align_bytes=LINE)
            nc.sync.dma_start(block[:], w[:, a * P : (a + 1) * P])
            return block

        def load_bias(a, queue):
            queue.dma_start(
                bias_runs[0:P:TURN, a * TURN : (a + 1) * TURN],
                b[a * P : (a + 1) * P, :].rearrange("(q i) o -> q (i o)", i=TURN),
            )

        load_bias(0, nc.scalar)
        rows = {0: load_rows(0)}
        weights = {0: load_weights(0)}
        moving = held.tile([P, PICKED], BF16, name="moving", align_bytes=LINE)
        nc.sync.dma_start(moving[:], x)
        offsets = held.tile([P, PICKED // 16], U16, name="offsets", align_bytes=LINE)
        nc.sync.dma_start(offsets[:], offs)
        for a in range(1, BLOCKS):
            rows[a] = load_rows(a)
            weights[a] = load_weights(a)
            load_bias(a, nc.sync)

        bias = held.tile([P, BLOCKS * TURN], F32, name="bias", align_bytes=64)
        for a in range(BLOCKS):
            nc.vector.transpose(bias[:, a * TURN : (a + 1) * TURN], bias_runs[:, a * TURN : (a + 1) * TURN])

        warm = held.tile([P, 1], F32, name="warm")
        nc.scalar.activation(warm[:], zeros[:, 0:1], GELU)

        spare = banks.tile([TURN, TOKENS], F32, name="spare")
        for i in range(IDLE_MATMULS):
            nc.tensor.matmul(spare[:], zeros[:], zeros[:, 0:1].to_broadcast([P, TOKENS]), start=True, stop=True)

        windows = [banks.tile([P, TOKENS], F32, name="window%d" % a) for a in range(BLOCKS)]
        for a in range(BLOCKS):
            if a == 0:
                for c, piece in rows[a].items():
                    nc.tensor.matmul(windows[a][:, c : c + piece.shape[1]], identity[:], piece[:], start=True, stop=True)
            else:
                cuts = BETWEEN_RUNS // (P // TURN) // PIECES
                for c, piece in rows[a].items():
                    units = piece.shape[1] // UNIT
                    edges = [UNIT * (units * i // cuts) for i in range(cuts + 1)]
                    for lo, hi in zip(edges[:-1], edges[1:]):
                        for q in range(0, P, TURN):
                            nc.tensor.matmul(
                                windows[a][q : q + TURN, c + lo : c + hi],
                                identity[:, q : q + TURN],
                                piece[:, lo:hi],
                                start=True,
                                stop=True,
                            )
            nc.tensor.matmul(
                windows[a][:].indirect(offsets[:]),
                weights[a][:],
                moving[:],
                start=True,
                stop=True,
            )
            for c in range(0, TOKENS, TOKENS // PIECES):
                columns = slice(c, c + TOKENS // PIECES)
                result = held.tile([P, TOKENS // PIECES], F32, name="result%d_%d" % (a, c), align_bytes=LINE)
                nc.scalar.activation(result[:], windows[a][:, columns], GELU, bias=bias[:, a * TURN : a * TURN + 1])
                nc.sync.dma_start(out[a * P : (a + 1) * P, columns], result[:])
